import numpy as np
import ml_dtypes


def mxq(x, axis, fmt="e4m3"):
    dtype, down = {"e4m3": (ml_dtypes.float8_e4m3fn, 7), "e5m2": (ml_dtypes.float8_e5m2, 14)}[fmt]
    v = np.moveaxis(np.asarray(x, np.float32).astype(ml_dtypes.bfloat16).astype(np.float64), axis, -1)
    blocks = v.reshape(v.shape[:-1] + (-1, 32))
    amax = np.abs(blocks).max(-1, keepdims=True)
    byte = np.maximum(np.where(amax > 0, np.frexp(amax)[1] - 1 + 127, 0) - down, 1)
    scale = np.exp2(byte - 127.0)
    codes = (blocks / scale).astype(np.float32).astype(dtype).astype(np.float64)
    return np.moveaxis((codes * scale).reshape(v.shape), -1, axis)


WIDE = False


def mx_kscale(k):
    if not WIDE:
        return np.ones(k)
    levels = np.array([10, -10, 5, -5, 0])
    if k % 512:
        return np.exp2(np.random.permutation(np.resize(levels, k // 32))).repeat(32)
    a = np.empty((k // 512, 16))
    for p in range(k // 512):
        a[p, :8] = np.random.permutation(np.resize(levels, 8))
        for g in range(8):
            far = levels[np.abs(levels - a[p, g]) >= 10]
            a[p, g + 8] = far[np.random.randint(len(far))]
    return np.exp2(a.ravel()).repeat(32)


BF16 = ml_dtypes.bfloat16


def bf(x):
    return np.asarray(x, np.float32).astype(BF16)


def f64(x):
    return np.asarray(x).astype(np.float64)


E2M1 = np.array([0.0, 0.5, 1.0, 1.5, 2.0, 3.0, 4.0, 6.0, -0.0, -0.5, -1.0, -1.5, -2.0, -3.0, -4.0, -6.0])


def pack_weight(w, fmt):
    k, n = w.shape
    w = f64(bf(w)).reshape(k // 32, 32, n)
    amax = np.abs(w).max(1)
    if fmt == "e4m3":
        byte = np.frexp(amax)[1] - 1 + 127 - 7
    else:
        mant, ex = np.frexp(amax / 6.0)
        byte = np.where(mant > 0.5, ex, ex - 1) + 127
    byte = np.clip(np.where(amax > 0, byte, 1), 1, 254)
    scaled = (w * np.exp2(127.0 - byte)[:, None, :]).reshape(k, n).astype(np.float32)
    by_word = np.ascontiguousarray(scaled.reshape(k // 512, 128, 4, n).transpose(0, 1, 3, 2))
    if fmt == "e4m3":
        words = by_word.astype(ml_dtypes.float8_e4m3fn).view(np.uint8)
    else:
        c = by_word.astype(ml_dtypes.float4_e2m1fn).view(np.uint8) & 0xF
        words = c[..., 0::2] | (c[..., 1::2] << 4)
    return np.ascontiguousarray(words), np.ascontiguousarray(byte.astype(np.uint8).reshape(k // 512, 16, n))


def unpack_weight(words, scales, fmt):
    g, p, n, _ = words.shape
    if fmt == "e4m3":
        vals = np.ascontiguousarray(words).view(ml_dtypes.float8_e4m3fn).astype(np.float64)
    else:
        nib = np.empty((g, p, n, 4), np.uint8)
        nib[..., 0::2] = words & 0xF
        nib[..., 1::2] = words >> 4
        vals = E2M1[nib]
    vals = vals * np.repeat(np.exp2(scales.astype(np.float64) - 127.0), 8, axis=1)[..., None]
    return vals.transpose(0, 1, 3, 2).reshape(g * 512, n)
def pack4(w):
    words, scales = pack_weight(w, "e2m1")
    return words.reshape(words.shape[0], 128, -1), scales


def unpack4(words, scales):
    return unpack_weight(words.reshape(words.shape[0], 128, -1, 2), scales, "e2m1")


def planes(Y):
    n, m = Y.shape
    b = f64(bf(Y)).reshape(n // 32, 32, m)
    amax = np.abs(b).max(1)
    byte = np.clip(np.where(amax > 0, np.frexp(amax)[1] - 1 + 127 - 7, 1), 1, 254)
    codes = (b * np.exp2(127.0 - byte)[:, None, :]).reshape(n, m).astype(np.float32).astype(ml_dtypes.float8_e4m3fn).view(np.uint8)
    words = codes.reshape(n // 512, 128, 4, m).transpose(0, 1, 3, 2)
    return np.ascontiguousarray(words), np.ascontiguousarray(byte.astype(np.uint8).reshape(n // 512, 16, m))


G, R, K, Q, N = 4, 1024, 512, 1024, 512

def setup_inputs():
    s = mx_kscale(K)
    t = mx_kscale(G * Q).reshape(G, Q)
    peptides = np.random.randn(R, K) * s
    contact = np.random.randn(G, K, Q) / np.sqrt(K) / s[None, :, None]
    contact_words, contact_scales = pack4(contact.reshape(G * K, Q))
    pocket_weight = np.exp(0.3 * np.random.randn(G, Q)) * t
    alleles = 2.0 * np.random.randn(G, N, Q) / np.sqrt(Q) / t[:, None, :]
    allele_bias = 0.5 * np.random.randn(G, N)
    expression = np.exp(0.8 * np.random.randn(G, N))
    return {"peptides": bf(peptides), "contact_words": contact_words, "contact_scales": contact_scales,
            "pocket_weight": bf(pocket_weight), "alleles": bf(alleles),
            "allele_bias": bf(allele_bias), "expression": bf(expression)}

def reference(peptides, contact_words, contact_scales, pocket_weight, alleles, allele_bias, expression):
    x = mxq(f64(peptides), 1, "e4m3")
    c = unpack4(contact_words, contact_scales).reshape(G, K, Q)
    h = np.tanh(x @ c) * f64(pocket_weight)[:, None, :]
    hq = mxq(h, 2, "e4m3")
    a = mxq(f64(alleles), 2, "e4m3")
    z = (hq @ a.swapaxes(1, 2)) + f64(allele_bias)[:, None, :]
    y = 1.0 / (1.0 + np.exp(-z)) * f64(expression)[:, None, :]
    Y = y.transpose(2, 0, 1).reshape(N, G * R)
    words, scales = planes(Y)
    return y, words, scales

@@ -1,0 +1,339 @@
+from contextlib import ExitStack
+
+import concourse.mybir as mybir
+from concourse.masks import make_identity
+
+G, R, K, Q, N = 4, 1024, 512, 1024, 512
+FLOPS = 2 * G * R * K * Q + 2 * G * R * Q * N
+
+F32 = mybir.dt.float32
+BF16 = mybir.dt.bfloat16
+I32 = mybir.dt.int32
+U32 = mybir.dt.uint32
+U8 = mybir.dt.uint8
+FP8X4 = mybir.dt.float8_e4m3fn_x4
+FP4X4 = mybir.dt.float4_e2m1fn_x4
+ACT = mybir.ActivationFunctionType
+ALU = mybir.AluOpType
+
+P = 128
+PACK = 4
+KP = P * PACK
+HALF = 512
+UNITS = G * R // HALF
+
+
+def tile_peptide_mhc_locus_affinity_k7_kernel(
+    tc, peptides, contact_words, contact_scales, pocket_weight, alleles, allele_bias, expression, out_0, out_1, out_2
+):
+    nc = tc.nc
+    with ExitStack() as ctx:
+        keep = ctx.enter_context(tc.tile_pool(name="keep", bufs=1))
+        work = ctx.enter_context(tc.tile_pool(name="work", bufs=2))
+        psum = ctx.enter_context(tc.psum_pool(name="psum", bufs=2))
+        ctx.enter_context(tc.manual_schedule())
+
+        ident = keep.tile([P, P], F32, name="ident")
+        make_identity(nc, ident[:])
+
+        x_raw = [keep.tile([P, 2, K], BF16, name="x_raw%d" % j) for j in range(4)]
+        c_raw = [keep.tile([P, 2 * Q], U8, name="c_raw%d" % i) for i in range(G)]
+        cs_raw0 = keep.tile([P, Q], U8, name="cs_raw0")
+        cs_raw1 = keep.tile([P, G - 1, Q], U8, name="cs_raw1")
+        a_raw = [keep.tile([P, PACK, Q], BF16, name="a_raw%d" % i) for i in range(G)]
+        w_raw = keep.tile([P, 2 * G, PACK], BF16, name="w_raw")
+        b_raw = keep.tile([P, G, PACK], BF16, name="b_raw")
+        e_raw = keep.tile([P, G, PACK], BF16, name="e_raw")
+        w_sb = keep.tile([P, 2 * G, PACK], F32, name="w_sb")
+        b_sb = keep.tile([P, G, PACK], F32, name="b_sb")
+        e_sb = keep.tile([P, G, PACK], F32, name="e_sb")
+        warm = keep.tile([P, 1], F32, name="warm")
+
+        x_codes = keep.tile([P, R], U32, name="x_codes", align_bytes=64)
+        x_scales = keep.tile([P, R], U8, name="x_scales", align_bytes=64)
+        c_codes = [keep.tile([P, 2 * Q], U8, name="c_codes%d" % i, align_bytes=64) for i in range(G)]
+        c_scales = [keep.tile([P, Q], U8, name="c_scales%d" % i, align_bytes=64) for i in range(G)]
+        a_codes = [keep.tile([P, 2 * N], U32, name="a_codes%d" % i, align_bytes=64) for i in range(G)]
+        a_scales = [keep.tile([P, 2 * N], U8, name="a_scales%d" % i, align_bytes=64) for i in range(G)]
+        y_scales = keep.tile([P, G * R], U8, name="y_scales", align_bytes=64)
+
+        nc.vector.memset(cs_raw0[:].bitcast(I32), 0)
+        nc.vector.memset(cs_raw1[:].rearrange("p g n -> p (g n)").bitcast(I32), 0)
+
+        def load_x(j):
+            rows = peptides[256 * j : 256 * (j + 1), :]
+            nc.sync.dma_start(out=x_raw[j][:], in_=rows.rearrange("(c p) k -> p c k", p=P))
+
+        def load_c(i):
+            nc.sync.dma_start(out=c_raw[i][:].bitcast(I32), in_=contact_words[i].bitcast(I32))
+
+        def load_a(i):
+            nc.sync.dma_start(out=a_raw[i][:], in_=alleles[i].rearrange("(m t) q -> m t q", t=PACK))
+
+        load_x(0)
+        load_c(0)
+        for quad in range(4):
+            nc.scalar.dma_start(
+                out=cs_raw0[32 * quad : 32 * quad + 4, :].bitcast(I32),
+                in_=contact_scales[0, 4 * quad : 4 * quad + 4, :].bitcast(I32),
+            )
+        load_x(1)
+        nc.sync.dma_start(out=w_raw[:], in_=pocket_weight.rearrange("i (g p t) -> p (i g) t", p=P, t=PACK))
+        load_a(0)
+        load_x(2)
+        load_x(3)
+        nc.sync.dma_start(out=b_raw[:], in_=allele_bias.rearrange("i (p t) -> p i t", t=PACK))
+        nc.sync.dma_start(out=e_raw[:], in_=expression.rearrange("i (p t) -> p i t", t=PACK))
+        load_c(1)
+        for quad in range(4):
+            nc.sync.dma_start(
+                out=cs_raw1[32 * quad : 32 * quad + 4, :, :].bitcast(I32),
+                in_=contact_scales[1:G, 4 * quad : 4 * quad + 4, :].rearrange("g r n -> r g n").bitcast(I32),
+            )
+        load_a(1)
+        load_c(2)
+        load_c(3)
+        load_a(2)
+        load_a(3)
+
+        nc.scalar.activation(out=warm[:], in_=ident[:, 0:1], func=ACT.Sigmoid)
+
+        x_bf = {}
+        a_bf = {}
+        th = {}
+        h_bf = {}
+        h_codes = {}
+        h_scales = {}
+        sg = {}
+        y = {}
+        y_bf = {}
+
+        def turn_words(words, first, grouped):
+            bank = psum.tile([P, 2, 2, P], F32, name="turn", tag="turn", bufs=2)
+            for x in range(2):
+                for u in range(2):
+                    lo = first[x]
+                    nc.tensor.transpose(bank[:, x, u, :], words[:, lo + u : lo + 256 : 2], ident[:])
+            nc.scalar.copy(
+                out=grouped.bitcast(F32).rearrange("p (x m u) -> p x m u", x=2, u=2),
+                in_=bank[:].rearrange("p x u m -> p x m u"),
+            )
+
+        def turn_x(j):
+            x_bf[j] = work.tile([P, 1024], BF16, name="x_bf", tag="x_bf", bufs=2, align_bytes=64)
+            words = x_raw[j][:].rearrange("p c k -> p (c k)").bitcast(F32)
+            turn_words(words, [0, 256], x_bf[j][:])
+
+        def quant_x(j):
+            cols = slice(256 * j, 256 * (j + 1))
+            nc.vector.quantize_mx(out=x_codes[:, cols].bitcast(FP8X4), scales=x_scales[:, cols], in_=x_bf[j][:])
+
+        def turn_a(i, g):
+            a_bf[i, g] = work.tile([P, 2048], BF16, name="a_bf", tag="a_bf", bufs=2, align_bytes=64)
+            words = a_raw[i][:].rearrange("p t q -> p (t q)").bitcast(F32)
+            for j in range(2):
+                first = [512 * (2 * j + x) + 256 * g for x in range(2)]
+                turn_words(words, first, a_bf[i, g][:, 1024 * j : 1024 * (j + 1)])
+
+        def quant_a(i, g):
+            cols = slice(N * g, N * (g + 1))
+            nc.vector.quantize_mx(out=a_codes[i][:, cols].bitcast(FP8X4), scales=a_scales[i][:, cols], in_=a_bf[i, g][:])
+
+        def sort_c_codes(i, g):
+            cols = slice(1024 * g, 1024 * (g + 1))
+            nc.vector.tensor_copy(
+                out=c_codes[i][:, cols].rearrange("p (t m b) -> p t m b", t=PACK, b=2),
+                in_=c_raw[i][:, cols].rearrange("p (m t b) -> p t m b", t=PACK, b=2),
+            )
+
+        def sort_c_scales(i, g):
+            cols = slice(KP * g, KP * (g + 1))
+            raw = cs_raw0[:, cols] if i == 0 else cs_raw1[:, i - 1, cols]
+            nc.vector.tensor_copy(
+                out=c_scales[i][:, cols].rearrange("p (t m) -> p t m", t=PACK),
+                in_=raw.rearrange("p (m t) -> p t m", t=PACK),
+            )
+
+        def stage1(u, g, pair):
+            i, h = divmod(u, 2)
+            th[u, g, pair] = work.tile([P, 2, KP], F32, name="th", tag="th", bufs=3)
+            for cc in range(2):
+                r0 = HALF * h + P * (2 * pair + cc)
+                bank = psum.tile([P, PACK, P], F32, name="s1", tag="s1", bufs=4)
+                for t in range(PACK):
+                    c0 = KP * g + P * t
+                    nc.tensor.matmul_mx(
+                        out=bank[:, t, :],
+                        lhsT=c_codes[i][:, 2 * c0 : 2 * (c0 + P)].bitcast(FP4X4),
+                        lhsT_scale=c_scales[i][:, c0 : c0 + P],
+                        rhs=x_codes[:, r0 : r0 + P].bitcast(FP8X4),
+                        rhs_scale=x_scales[:, r0 : r0 + P],
+                        start=True,
+                        stop=True,
+                    )
+                nc.scalar.activation(
+                    out=th[u, g, pair][:, cc, :].rearrange("p (r t) -> p r t", t=PACK),
+                    in_=bank[:].rearrange("p t r -> p r t"),
+                    func=ACT.Tanh,
+                )
+
+        def weigh(u, g, pair):
+            i = u // 2
+            if pair == 0:
+                h_bf[u, g] = work.tile([P, 2048], BF16, name="h_bf", tag="h_bf", bufs=2, align_bytes=64)
+            nc.vector.tensor_tensor(
+                out=h_bf[u, g][:, 1024 * pair : 1024 * (pair + 1)].rearrange("p (r t) -> p r t", t=PACK),
+                in0=th[u, g, pair][:].rearrange("p c (r t) -> p (c r) t", t=PACK),
+                in1=w_sb[:, 2 * i + g : 2 * i + g + 1, :].to_broadcast([P, 2 * P, PACK]),
+                op=ALU.mult,
+            )
+
+        def quant_h(u, g):
+            h_codes[u, g] = work.tile([P, HALF], U32, name="h_codes", tag="h_codes", bufs=4, align_bytes=64)
+            h_scales[u, g] = work.tile([P, HALF], U8, name="h_scales", tag="h_scales", bufs=4, align_bytes=64)
+            nc.vector.quantize_mx(out=h_codes[u, g][:].bitcast(FP8X4), scales=h_scales[u, g][:], in_=h_bf[u, g][:])
+
+        def stage2(u, t):
+            i = u // 2
+            if t == 0:
+                sg[u] = work.tile([P, PACK, HALF], F32, name="sg", tag="sg", bufs=2)
+            bank = psum.tile([P, HALF], F32, name="s2", tag="s2", bufs=2)
+            for g in range(2):
+                c0 = N * g + P * t
+                nc.tensor.matmul_mx(
+                    out=bank[:],
+                    lhsT=a_codes[i][:, c0 : c0 + P].bitcast(FP8X4),
+                    lhsT_scale=a_scales[i][:, c0 : c0 + P],
+                    rhs=h_codes[u, g][:].bitcast(FP8X4),
+                    rhs_scale=h_scales[u, g][:],
+                    start=(g == 0),
+                    stop=(g == 1),
+                )
+            nc.scalar.activation(out=sg[u][:, t, :], in_=bank[:], func=ACT.Sigmoid, bias=b_sb[:, i, t : t + 1])
+
+        def express(u, t):
+            i = u // 2
+            if t == 0:
+                y[u] = work.tile([P, PACK, HALF], F32, name="y", tag="y", bufs=2)
+            nc.vector.tensor_scalar(
+                out=y[u][:, t, :], in0=sg[u][:, t, :], scalar1=e_sb[:, i, t : t + 1], scalar2=None, op0=ALU.mult
+            )
+
+        def group_y(u):
+            y_bf[u] = work.tile([P, 2048], BF16, name="y_bf", tag="y_bf", bufs=2, align_bytes=64)
+            nc.vector.tensor_copy(
+                out=y_bf[u][:].rearrange("p (c j t) -> p c t j", j=4, t=PACK),
+                in_=y[u][:].rearrange("p t (c j) -> p c t j", j=4),
+            )
+
+        def quant_y(u):
+            codes = work.tile([P, HALF], U32, name="y_codes", tag="y_codes", bufs=2, align_bytes=64)
+            cols = slice(HALF * u, HALF * (u + 1))
+            nc.vector.quantize_mx(out=codes[:].bitcast(FP8X4), scales=y_scales[:, cols], in_=y_bf[u][:])
+            words = out_1[0].rearrange("p m t -> p (m t)")[:, PACK * HALF * u : PACK * HALF * (u + 1)]
+            nc.sync.dma_start(out=words.bitcast(I32), in_=codes[:].bitcast(I32))
+
+        def store_scales(lo, hi):
+            for quad in range(4):
+                nc.sync.dma_start(
+                    out=out_2[0, 4 * quad : 4 * quad + 4, lo:hi].bitcast(I32),
+                    in_=y_scales[32 * quad : 32 * quad + 4, lo:hi].bitcast(I32),
+                )
+
+        def turn_y(u, pair):
+            i, h = divmod(u, 2)
+            rows = work.tile([P, 2, N], F32, name="rows", tag="rows", bufs=4)
+            for cc in range(2):
+                c = 2 * pair + cc
+                bank = psum.tile([P, PACK, P], F32, name="turn", tag="turn", bufs=2)
+                for t in range(PACK):
+                    nc.tensor.transpose(bank[:, t, :], y[u][:, t, P * c : P * (c + 1)], ident[:])
+                nc.scalar.copy(
+                    out=rows[:, cc, :].rearrange("r (p t) -> r p t", t=PACK), in_=bank[:].rearrange("r t p -> r p t")
+                )
+            r0 = HALF * h + 2 * P * pair
+            nc.sync.dma_start(out=out_0[i, r0 : r0 + 2 * P, :].rearrange("(c p) a -> p c a", p=P), in_=rows[:])
+
+        sort_c_codes(0, 0)
+        turn_x(0)
+        sort_c_scales(0, 0)
+        quant_x(0)
+        turn_x(1)
+        sort_c_codes(0, 1)
+        quant_x(1)
+        nc.vector.tensor_copy(out=w_sb[:], in_=w_raw[:])
+        sort_c_scales(0, 1)
+
+        stage1(0, 0, 0)
+        stage1(0, 0, 1)
+        weigh(0, 0, 0)
+        turn_a(0, 0)
+        weigh(0, 0, 1)
+        stage1(0, 1, 0)
+        quant_a(0, 0)
+        quant_h(0, 0)
+        turn_x(2)
+        turn_x(3)
+        weigh(0, 1, 0)
+        quant_x(2)
+        quant_x(3)
+        nc.vector.tensor_copy(out=b_sb[:], in_=b_raw[:])
+        nc.vector.tensor_copy(out=e_sb[:], in_=e_raw[:])
+        stage1(0, 1, 1)
+        turn_a(0, 1)
+        sort_c_codes(1, 0)
+        sort_c_scales(1, 0)
+
+        for s in range(1, UNITS):
+            nxt_a = divmod(s + 1, 2)
+            nxt_c = divmod(s + 2, 2)
+            weigh(s - 1, 1, 1)
+            if s == 1:
+                quant_a(0, 1)
+            else:
+                quant_y(s - 2)
+            quant_h(s - 1, 1)
+            stage1(s, 0, 0)
+            weigh(s, 0, 0)
+            if nxt_a[0] < G:
+                turn_a(*nxt_a)
+                quant_a(*nxt_a)
+            stage1(s, 0, 1)
+            weigh(s, 0, 1)
+            stage2(s - 1, 0)
+            stage2(s - 1, 1)
+            express(s - 1, 0)
+            express(s - 1, 1)
+            quant_h(s, 0)
+            if nxt_c[0] < G:
+                sort_c_scales(*nxt_c)
+            if s >= 2:
+                turn_y(s - 2, 0)
+            stage1(s, 1, 0)
+            weigh(s, 1, 0)
+            stage2(s - 1, 2)
+            stage2(s - 1, 3)
+            if s >= 2:
+                turn_y(s - 2, 1)
+            express(s - 1, 2)
+            express(s - 1, 3)
+            if nxt_c[0] < G:
+                sort_c_codes(*nxt_c)
+            group_y(s - 1)
+            stage1(s, 1, 1)
+
+        last = UNITS - 1
+        weigh(last, 1, 1)
+        quant_y(last - 1)
+        quant_h(last, 1)
+        store_scales(0, HALF * last)
+        turn_y(last - 1, 0)
+        turn_y(last - 1, 1)
+        for t in range(PACK):
+            stage2(last, t)
+            express(last, t)
+        group_y(last)
+        turn_y(last, 0)
+        quant_y(last)
+        store_scales(HALF * last, HALF * UNITS)
+        turn_y(last, 1)

@@ -41,10 +41,11 @@ def tile_peptide_mhc_locus_affinity_k7_kernel(
         cs_raw0 = keep.tile([P, Q], U8, name="cs_raw0")
         cs_raw1 = keep.tile([P, G - 1, Q], U8, name="cs_raw1")
         a_raw = [keep.tile([P, PACK, Q], BF16, name="a_raw%d" % i) for i in range(G)]
-        w_raw = keep.tile([P, 2 * G, PACK], BF16, name="w_raw")
+        w_raw = keep.tile([P, KP], BF16, name="w_raw")
+        w_rows = keep.tile([P, KP], F32, name="w_rows")
         b_raw = keep.tile([P, G, PACK], BF16, name="b_raw")
         e_raw = keep.tile([P, G, PACK], BF16, name="e_raw")
-        w_sb = keep.tile([P, 2 * G, PACK], F32, name="w_sb")
+        w_ps = psum.tile([P, P, PACK], F32, name="w_ps", tag="w_ps", bufs=1)
         b_sb = keep.tile([P, G, PACK], F32, name="b_sb")
         e_sb = keep.tile([P, G, PACK], F32, name="e_sb")
         warm = keep.tile([P, 1], F32, name="warm")
@@ -55,9 +56,11 @@ def tile_peptide_mhc_locus_affinity_k7_kernel(
         c_scales = [keep.tile([P, Q], U8, name="c_scales%d" % i, align_bytes=64) for i in range(G)]
         a_codes = [keep.tile([P, 2 * N], U32, name="a_codes%d" % i, align_bytes=64) for i in range(G)]
         a_scales = [keep.tile([P, 2 * N], U8, name="a_scales%d" % i, align_bytes=64) for i in range(G)]
+        y_codes = keep.tile([P, G * R], U32, name="y_codes", align_bytes=64)
         y_scales = keep.tile([P, G * R], U8, name="y_scales", align_bytes=64)
 
         nc.vector.memset(cs_raw0[:].bitcast(I32), 0)
+        nc.vector.memset(w_raw[:], 0.0)
         nc.vector.memset(cs_raw1[:].rearrange("p g n -> p (g n)").bitcast(I32), 0)
 
         def load_x(j):
@@ -78,18 +81,18 @@ def tile_peptide_mhc_locus_affinity_k7_kernel(
                 in_=contact_scales[0, 4 * quad : 4 * quad + 4, :].bitcast(I32),
             )
         load_x(1)
-        nc.sync.dma_start(out=w_raw[:], in_=pocket_weight.rearrange("i (g p t) -> p (i g) t", p=P, t=PACK))
+        nc.sync.dma_start(out=w_raw[0 : 2 * G, :], in_=pocket_weight.rearrange("i (g q) -> (i g) q", g=2))
         load_a(0)
-        load_x(2)
-        load_x(3)
-        nc.sync.dma_start(out=b_raw[:], in_=allele_bias.rearrange("i (p t) -> p i t", t=PACK))
-        nc.sync.dma_start(out=e_raw[:], in_=expression.rearrange("i (p t) -> p i t", t=PACK))
         load_c(1)
         for quad in range(4):
             nc.sync.dma_start(
                 out=cs_raw1[32 * quad : 32 * quad + 4, :, :].bitcast(I32),
                 in_=contact_scales[1:G, 4 * quad : 4 * quad + 4, :].rearrange("g r n -> r g n").bitcast(I32),
             )
+        load_x(2)
+        load_x(3)
+        nc.sync.dma_start(out=b_raw[:], in_=allele_bias.rearrange("i (p t) -> p i t", t=PACK))
+        nc.sync.dma_start(out=e_raw[:], in_=expression.rearrange("i (p t) -> p i t", t=PACK))
         load_a(1)
         load_c(2)
         load_c(3)
@@ -108,32 +111,39 @@ def tile_peptide_mhc_locus_affinity_k7_kernel(
         y = {}
         y_bf = {}
 
-        def turn_words(words, first, grouped):
-            bank = psum.tile([P, 2, 2, P], F32, name="turn", tag="turn", bufs=2)
+        def leave(on_vector, out, in_):
+            if on_vector:
+                nc.vector.tensor_copy(out=out, in_=in_)
+            else:
+                nc.scalar.copy(out=out, in_=in_)
+
+        def turn_words(words, first, grouped, on_vector):
+            bank = psum.tile([P, 2, 2, P], F32, name="bank", tag="bank", bufs=7)
             for x in range(2):
                 for u in range(2):
                     lo = first[x]
                     nc.tensor.transpose(bank[:, x, u, :], words[:, lo + u : lo + 256 : 2], ident[:])
-            nc.scalar.copy(
-                out=grouped.bitcast(F32).rearrange("p (x m u) -> p x m u", x=2, u=2),
-                in_=bank[:].rearrange("p x u m -> p x m u"),
+            leave(
+                on_vector,
+                grouped.bitcast(F32).rearrange("p (x m u) -> p x m u", x=2, u=2),
+                bank[:].rearrange("p x u m -> p x m u"),
             )
 
         def turn_x(j):
             x_bf[j] = work.tile([P, 1024], BF16, name="x_bf", tag="x_bf", bufs=2, align_bytes=64)
             words = x_raw[j][:].rearrange("p c k -> p (c k)").bitcast(F32)
-            turn_words(words, [0, 256], x_bf[j][:])
+            turn_words(words, [0, 256], x_bf[j][:], False)
 
         def quant_x(j):
             cols = slice(256 * j, 256 * (j + 1))
             nc.vector.quantize_mx(out=x_codes[:, cols].bitcast(FP8X4), scales=x_scales[:, cols], in_=x_bf[j][:])
 
-        def turn_a(i, g):
+        def turn_a(i, g, on_vector):
             a_bf[i, g] = work.tile([P, 2048], BF16, name="a_bf", tag="a_bf", bufs=2, align_bytes=64)
             words = a_raw[i][:].rearrange("p t q -> p (t q)").bitcast(F32)
             for j in range(2):
                 first = [512 * (2 * j + x) + 256 * g for x in range(2)]
-                turn_words(words, first, a_bf[i, g][:, 1024 * j : 1024 * (j + 1)])
+                turn_words(words, first, a_bf[i, g][:, 1024 * j : 1024 * (j + 1)], on_vector)
 
         def quant_a(i, g):
             cols = slice(N * g, N * (g + 1))
@@ -156,35 +166,36 @@ def tile_peptide_mhc_locus_affinity_k7_kernel(
 
         def stage1(u, g, pair):
             i, h = divmod(u, 2)
-            th[u, g, pair] = work.tile([P, 2, KP], F32, name="th", tag="th", bufs=3)
-            for cc in range(2):
-                r0 = HALF * h + P * (2 * pair + cc)
-                bank = psum.tile([P, PACK, P], F32, name="s1", tag="s1", bufs=4)
-                for t in range(PACK):
-                    c0 = KP * g + P * t
+            th[u, g, pair] = work.tile([P, 2, KP], F32, name="th", tag="th", bufs=5)
+            r0 = HALF * h + 2 * P * pair
+            for hi in range(2):
+                bank = psum.tile([P, 2, 2 * P], F32, name="bank", tag="bank", bufs=7)
+                for lo in range(2):
+                    c0 = KP * g + P * (2 * hi + lo)
                     nc.tensor.matmul_mx(
-                        out=bank[:, t, :],
+                        out=bank[:, lo, :],
                         lhsT=c_codes[i][:, 2 * c0 : 2 * (c0 + P)].bitcast(FP4X4),
                         lhsT_scale=c_scales[i][:, c0 : c0 + P],
-                        rhs=x_codes[:, r0 : r0 + P].bitcast(FP8X4),
-                        rhs_scale=x_scales[:, r0 : r0 + P],
+                        rhs=x_codes[:, r0 : r0 + 2 * P].bitcast(FP8X4),
+                        rhs_scale=x_scales[:, r0 : r0 + 2 * P],
                         start=True,
                         stop=True,
                     )
                 nc.scalar.activation(
-                    out=th[u, g, pair][:, cc, :].rearrange("p (r t) -> p r t", t=PACK),
-                    in_=bank[:].rearrange("p t r -> p r t"),
+                    out=th[u, g, pair][:, hi, :].rearrange("p (r e) -> p r e", e=2),
+                    in_=bank[:].rearrange("p e r -> p r e"),
                     func=ACT.Tanh,
                 )
 
         def weigh(u, g, pair):
             i = u // 2
             if pair == 0:
-                h_bf[u, g] = work.tile([P, 2048], BF16, name="h_bf", tag="h_bf", bufs=2, align_bytes=64)
+                h_bf[u, g] = work.tile([P, 2048], BF16, name="h_bf", tag="h_bf", bufs=3, align_bytes=64)
+            row = 2 * i + g
             nc.vector.tensor_tensor(
-                out=h_bf[u, g][:, 1024 * pair : 1024 * (pair + 1)].rearrange("p (r t) -> p r t", t=PACK),
-                in0=th[u, g, pair][:].rearrange("p c (r t) -> p (c r) t", t=PACK),
-                in1=w_sb[:, 2 * i + g : 2 * i + g + 1, :].to_broadcast([P, 2 * P, PACK]),
+                out=h_bf[u, g][:, 1024 * pair : 1024 * (pair + 1)].rearrange("p (r h e) -> p r h e", h=2, e=2),
+                in0=th[u, g, pair][:].rearrange("p h (r e) -> p r h e", e=2),
+                in1=w_ps[:, row : row + 1, :].rearrange("p o (h e) -> p o h e", e=2).to_broadcast([P, 2 * P, 2, 2]),
                 op=ALU.mult,
             )
 
@@ -197,7 +208,7 @@ def tile_peptide_mhc_locus_affinity_k7_kernel(
             i = u // 2
             if t == 0:
                 sg[u] = work.tile([P, PACK, HALF], F32, name="sg", tag="sg", bufs=2)
-            bank = psum.tile([P, HALF], F32, name="s2", tag="s2", bufs=2)
+            bank = psum.tile([P, HALF], F32, name="bank", tag="bank", bufs=7)
             for g in range(2):
                 c0 = N * g + P * t
                 nc.tensor.matmul_mx(
@@ -211,27 +222,39 @@ def tile_peptide_mhc_locus_affinity_k7_kernel(
                 )
             nc.scalar.activation(out=sg[u][:, t, :], in_=bank[:], func=ACT.Sigmoid, bias=b_sb[:, i, t : t + 1])
 
-        def express(u, t):
+        def express(u, t, on_vector):
             i = u // 2
             if t == 0:
-                y[u] = work.tile([P, PACK, HALF], F32, name="y", tag="y", bufs=2)
-            nc.vector.tensor_scalar(
-                out=y[u][:, t, :], in0=sg[u][:, t, :], scalar1=e_sb[:, i, t : t + 1], scalar2=None, op0=ALU.mult
+                y[u] = work.tile([P, PACK, HALF], F32, name="y", tag="y", bufs=3)
+            engine = nc.vector if on_vector else nc.gpsimd
+            engine.tensor_scalar(
+                out=y[u][:, t, :], in0=sg[u][:, t, :], scalar1=e_sb[:, i, t : t + 1], scalar2=0.0, op0=ALU.mult, op1=ALU.add
             )
 
-        def group_y(u):
+        def group_y(u, on_vector):
             y_bf[u] = work.tile([P, 2048], BF16, name="y_bf", tag="y_bf", bufs=2, align_bytes=64)
-            nc.vector.tensor_copy(
-                out=y_bf[u][:].rearrange("p (c j t) -> p c t j", j=4, t=PACK),
-                in_=y[u][:].rearrange("p t (c j) -> p c t j", j=4),
-            )
+            if on_vector:
+                nc.vector.tensor_copy(
+                    out=y_bf[u][:].rearrange("p (r t) -> p r t", t=PACK), in_=y[u][:].rearrange("p t r -> p r t")
+                )
+            else:
+                for c in range(4):
+                    nc.gpsimd.tensor_scalar(
+                        out=y_bf[u][:, KP * c : KP * (c + 1)].rearrange("p (r t) -> p r t", t=PACK),
+                        in0=y[u][:, :, P * c : P * (c + 1)].rearrange("p t r -> p r t"),
+                        scalar1=1.0,
+                        scalar2=0.0,
+                        op0=ALU.mult,
+                        op1=ALU.add,
+                    )
 
         def quant_y(u):
-            codes = work.tile([P, HALF], U32, name="y_codes", tag="y_codes", bufs=2, align_bytes=64)
             cols = slice(HALF * u, HALF * (u + 1))
-            nc.vector.quantize_mx(out=codes[:].bitcast(FP8X4), scales=y_scales[:, cols], in_=y_bf[u][:])
-            words = out_1[0].rearrange("p m t -> p (m t)")[:, PACK * HALF * u : PACK * HALF * (u + 1)]
-            nc.sync.dma_start(out=words.bitcast(I32), in_=codes[:].bitcast(I32))
+            nc.vector.quantize_mx(out=y_codes[:, cols].bitcast(FP8X4), scales=y_scales[:, cols], in_=y_bf[u][:])
+
+        def store_words(lo, hi):
+            words = out_1[0].rearrange("p m t -> p (m t)")[:, PACK * lo : PACK * hi]
+            nc.sync.dma_start(out=words.bitcast(I32), in_=y_codes[:, lo:hi].bitcast(I32))
 
         def store_scales(lo, hi):
             for quad in range(4):
@@ -240,100 +263,113 @@ def tile_peptide_mhc_locus_affinity_k7_kernel(
                     in_=y_scales[32 * quad : 32 * quad + 4, lo:hi].bitcast(I32),
                 )
 
-        def turn_y(u, pair):
+        def turn_y(u, chunks, on_vector):
             i, h = divmod(u, 2)
-            rows = work.tile([P, 2, N], F32, name="rows", tag="rows", bufs=4)
-            for cc in range(2):
-                c = 2 * pair + cc
-                bank = psum.tile([P, PACK, P], F32, name="turn", tag="turn", bufs=2)
+            rows = work.tile([P, len(chunks), N], F32, name="rows", tag="rows", bufs=4)
+            for cc, c in enumerate(chunks):
+                bank = psum.tile([P, PACK, P], F32, name="bank", tag="bank", bufs=7)
                 for t in range(PACK):
                     nc.tensor.transpose(bank[:, t, :], y[u][:, t, P * c : P * (c + 1)], ident[:])
-                nc.scalar.copy(
-                    out=rows[:, cc, :].rearrange("r (p t) -> r p t", t=PACK), in_=bank[:].rearrange("r t p -> r p t")
+                leave(
+                    on_vector[cc], rows[:, cc, :].rearrange("r (p t) -> r p t", t=PACK), bank[:].rearrange("r t p -> r p t")
                 )
-            r0 = HALF * h + 2 * P * pair
-            nc.sync.dma_start(out=out_0[i, r0 : r0 + 2 * P, :].rearrange("(c p) a -> p c a", p=P), in_=rows[:])
+            r0 = HALF * h + P * chunks[0]
+            dst = out_0[i, r0 : r0 + P * len(chunks), :]
+            nc.sync.dma_start(out=dst.rearrange("(c p) a -> p c a", p=P), in_=rows[:])
 
         sort_c_codes(0, 0)
         turn_x(0)
         sort_c_scales(0, 0)
         quant_x(0)
         turn_x(1)
-        sort_c_codes(0, 1)
+        nc.vector.tensor_copy(out=w_rows[:], in_=w_raw[:])
         quant_x(1)
-        nc.vector.tensor_copy(out=w_sb[:], in_=w_raw[:])
+        sort_c_codes(0, 1)
         sort_c_scales(0, 1)
 
         stage1(0, 0, 0)
         stage1(0, 0, 1)
+        for t in range(PACK):
+            nc.tensor.transpose(w_ps[:, :, t], w_rows[:, t:KP:PACK], ident[:])
+        sort_c_codes(1, 0)
         weigh(0, 0, 0)
-        turn_a(0, 0)
-        weigh(0, 0, 1)
         stage1(0, 1, 0)
-        quant_a(0, 0)
-        quant_h(0, 0)
+        weigh(0, 0, 1)
+        turn_a(0, 0, False)
         turn_x(2)
         turn_x(3)
         weigh(0, 1, 0)
         quant_x(2)
+        quant_h(0, 0)
         quant_x(3)
+        sort_c_scales(1, 0)
+        quant_a(0, 0)
+        stage1(0, 1, 1)
+        turn_a(0, 1, False)
+        weigh(0, 1, 1)
         nc.vector.tensor_copy(out=b_sb[:], in_=b_raw[:])
         nc.vector.tensor_copy(out=e_sb[:], in_=e_raw[:])
-        stage1(0, 1, 1)
-        turn_a(0, 1)
-        sort_c_codes(1, 0)
-        sort_c_scales(1, 0)
-
-        for s in range(1, UNITS):
-            nxt_a = divmod(s + 1, 2)
-            nxt_c = divmod(s + 2, 2)
-            weigh(s - 1, 1, 1)
-            if s == 1:
-                quant_a(0, 1)
-            else:
-                quant_y(s - 2)
-            quant_h(s - 1, 1)
-            stage1(s, 0, 0)
-            weigh(s, 0, 0)
-            if nxt_a[0] < G:
-                turn_a(*nxt_a)
-                quant_a(*nxt_a)
-            stage1(s, 0, 1)
-            weigh(s, 0, 1)
-            stage2(s - 1, 0)
-            stage2(s - 1, 1)
-            express(s - 1, 0)
-            express(s - 1, 1)
-            quant_h(s, 0)
-            if nxt_c[0] < G:
-                sort_c_scales(*nxt_c)
-            if s >= 2:
-                turn_y(s - 2, 0)
-            stage1(s, 1, 0)
-            weigh(s, 1, 0)
-            stage2(s - 1, 2)
-            stage2(s - 1, 3)
-            if s >= 2:
-                turn_y(s - 2, 1)
-            express(s - 1, 2)
-            express(s - 1, 3)
-            if nxt_c[0] < G:
-                sort_c_codes(*nxt_c)
-            group_y(s - 1)
-            stage1(s, 1, 1)
+        quant_h(0, 1)
+        quant_a(0, 1)
 
         last = UNITS - 1
-        weigh(last, 1, 1)
+        for s in range(1, UNITS):
+            nxt_a = divmod(s + 1, 2)
+            nxt_c = divmod(s + 3, 2)
+            stage1(s, 0, 0)
+            weigh(s, 0, 0)
+            stage1(s, 0, 1)
+            weigh(s, 0, 1)
+            stage1(s, 1, 0)
+            weigh(s, 1, 0)
+            if s >= 2:
+                group_y(s - 2, False)
+            stage2(s - 1, 0)
+            express(s - 1, 0, False)
+            if s == 1:
+                turn_a(*nxt_a, False)
+                sort_c_codes(1, 1)
+                sort_c_scales(1, 1)
+            else:
+                turn_y(s - 2, [0, 1], [False, False])
+            stage2(s - 1, 1)
+            express(s - 1, 1, False)
+            if 2 <= s < last:
+                turn_a(*nxt_a, True)
+            stage1(s, 1, 1)
+            weigh(s, 1, 1)
+            stage2(s - 1, 2)
+            express(s - 1, 2, False)
+            if s >= 2:
+                turn_y(s - 2, [2, 3], [False, False])
+            stage2(s - 1, 3)
+            quant_h(s, 0)
+            quant_h(s, 1)
+            if s < last:
+                quant_a(*nxt_a)
+            if s >= 2:
+                quant_y(s - 2)
+                store_words(HALF * (s - 2), HALF * (s - 1))
+            express(s - 1, 3, True)
+            if nxt_c[0] < G:
+                sort_c_codes(*nxt_c)
+                sort_c_scales(*nxt_c)
+
+        store_scales(0, HALF * (last - 1))
+        group_y(last - 1, True)
+        stage2(last, 0)
+        turn_y(last - 1, [0, 1], [False, False])
+        stage2(last, 1)
+        stage2(last, 2)
+        stage2(last, 3)
         quant_y(last - 1)
-        quant_h(last, 1)
-        store_scales(0, HALF * last)
-        turn_y(last - 1, 0)
-        turn_y(last - 1, 1)
-        for t in range(PACK):
-            stage2(last, t)
-            express(last, t)
-        group_y(last)
-        turn_y(last, 0)
+        store_words(HALF * (last - 1), HALF * last)
+        for t in range(4):
+            express(last, t, True)
+        turn_y(last - 1, [2, 3], [False, False])
+        group_y(last, True)
+        turn_y(last, [0, 1], [False, False])
         quant_y(last)
-        store_scales(HALF * last, HALF * UNITS)
-        turn_y(last, 1)
+        store_words(HALF * last, HALF * UNITS)
+        store_scales(HALF * (last - 1), HALF * UNITS)
+        turn_y(last, [2, 3], [False, True])

@@ -38,9 +38,8 @@ def tile_peptide_mhc_locus_affinity_k7_kernel(
 
         x_raw = [keep.tile([P, 2, K], BF16, name="x_raw%d" % j) for j in range(4)]
         c_raw = [keep.tile([P, 2 * Q], U8, name="c_raw%d" % i) for i in range(G)]
-        cs_raw0 = keep.tile([P, Q], U8, name="cs_raw0")
-        cs_raw1 = keep.tile([P, G - 1, Q], U8, name="cs_raw1")
-        a_raw = [keep.tile([P, PACK, Q], BF16, name="a_raw%d" % i) for i in range(G)]
+        cs_raw = keep.tile([P, Q], U8, name="cs_raw")
+        a_raw = {}
         w_raw = keep.tile([P, KP], BF16, name="w_raw")
         w_rows = keep.tile([P, KP], F32, name="w_rows")
         b_raw = keep.tile([P, G, PACK], BF16, name="b_raw")
@@ -59,9 +58,10 @@ def tile_peptide_mhc_locus_affinity_k7_kernel(
         y_codes = keep.tile([P, G * R], U32, name="y_codes", align_bytes=64)
         y_scales = keep.tile([P, G * R], U8, name="y_scales", align_bytes=64)
 
-        nc.vector.memset(cs_raw0[:].bitcast(I32), 0)
+        nc.vector.memset(cs_raw[:].bitcast(I32), 0)
         nc.vector.memset(w_raw[:], 0.0)
-        nc.vector.memset(cs_raw1[:].rearrange("p g n -> p (g n)").bitcast(I32), 0)
+        for i in range(1, G):
+            nc.vector.memset(c_scales[i][:].bitcast(I32), 0)
 
         def load_x(j):
             rows = peptides[256 * j : 256 * (j + 1), :]
@@ -71,33 +71,25 @@ def tile_peptide_mhc_locus_affinity_k7_kernel(
             nc.sync.dma_start(out=c_raw[i][:].bitcast(I32), in_=contact_words[i].bitcast(I32))
 
         def load_a(i):
+            a_raw[i] = work.tile([P, PACK, Q], BF16, name="a_raw", tag="a_raw", bufs=3)
             nc.sync.dma_start(out=a_raw[i][:], in_=alleles[i].rearrange("(m t) q -> m t q", t=PACK))
 
         load_x(0)
         load_c(0)
         for quad in range(4):
             nc.scalar.dma_start(
-                out=cs_raw0[32 * quad : 32 * quad + 4, :].bitcast(I32),
-                in_=contact_scales[0, 4 * quad : 4 * quad + 4, :].bitcast(I32),
+                out=cs_raw[32 * quad : 32 * quad + 4 * G, :].bitcast(I32),
+                in_=contact_scales[:, 4 * quad : 4 * quad + 4, :].bitcast(I32),
             )
         load_x(1)
         nc.sync.dma_start(out=w_raw[0 : 2 * G, :], in_=pocket_weight.rearrange("i (g q) -> (i g) q", g=2))
         load_a(0)
         load_c(1)
-        for quad in range(4):
-            nc.sync.dma_start(
-                out=cs_raw1[32 * quad : 32 * quad + 4, :, :].bitcast(I32),
-                in_=contact_scales[1:G, 4 * quad : 4 * quad + 4, :].rearrange("g r n -> r g n").bitcast(I32),
-            )
         load_x(2)
         load_x(3)
         nc.sync.dma_start(out=b_raw[:], in_=allele_bias.rearrange("i (p t) -> p i t", t=PACK))
         nc.sync.dma_start(out=e_raw[:], in_=expression.rearrange("i (p t) -> p i t", t=PACK))
         load_a(1)
-        load_c(2)
-        load_c(3)
-        load_a(2)
-        load_a(3)
 
         nc.scalar.activation(out=warm[:], in_=ident[:, 0:1], func=ACT.Sigmoid)
 
@@ -107,6 +99,7 @@ def tile_peptide_mhc_locus_affinity_k7_kernel(
         h_bf = {}
         h_codes = {}
         h_scales = {}
+        z = {}
         sg = {}
         y = {}
         y_bf = {}
@@ -117,22 +110,26 @@ def tile_peptide_mhc_locus_affinity_k7_kernel(
             else:
                 nc.scalar.copy(out=out, in_=in_)
 
-        def turn_words(words, first, grouped, on_vector):
-            bank = psum.tile([P, 2, 2, P], F32, name="bank", tag="bank", bufs=7)
-            for x in range(2):
-                for u in range(2):
-                    lo = first[x]
-                    nc.tensor.transpose(bank[:, x, u, :], words[:, lo + u : lo + 256 : 2], ident[:])
-            leave(
-                on_vector,
-                grouped.bitcast(F32).rearrange("p (x m u) -> p x m u", x=2, u=2),
-                bank[:].rearrange("p x u m -> p x m u"),
-            )
+        def turn_words(words, firsts, grouped, on_vector):
+            banks = []
+            for j in range(len(firsts) // 2):
+                bank = psum.tile([P, 2, 2, P], F32, name="bank", tag="bank", bufs=7)
+                for x in range(2):
+                    for u in range(2):
+                        lo = firsts[2 * j + x]
+                        nc.tensor.transpose(bank[:, x, u, :], words[:, lo + u : lo + 256 : 2], ident[:])
+                banks.append(bank)
+            for j in reversed(range(len(banks))):
+                leave(
+                    on_vector,
+                    grouped[:, 1024 * j : 1024 * (j + 1)].bitcast(F32).rearrange("p (x m u) -> p x m u", x=2, u=2),
+                    banks[j][:].rearrange("p x u m -> p x m u"),
+                )
 
         def turn_x(j):
             x_bf[j] = work.tile([P, 1024], BF16, name="x_bf", tag="x_bf", bufs=2, align_bytes=64)
             words = x_raw[j][:].rearrange("p c k -> p (c k)").bitcast(F32)
-            turn_words(words, [0, 256], x_bf[j][:], False)
+            turn_words(words, [0, 256], x_bf[j], False)
 
         def quant_x(j):
             cols = slice(256 * j, 256 * (j + 1))
@@ -141,9 +138,7 @@ def tile_peptide_mhc_locus_affinity_k7_kernel(
         def turn_a(i, g, on_vector):
             a_bf[i, g] = work.tile([P, 2048], BF16, name="a_bf", tag="a_bf", bufs=2, align_bytes=64)
             words = a_raw[i][:].rearrange("p t q -> p (t q)").bitcast(F32)
-            for j in range(2):
-                first = [512 * (2 * j + x) + 256 * g for x in range(2)]
-                turn_words(words, first, a_bf[i, g][:, 1024 * j : 1024 * (j + 1)], on_vector)
+            turn_words(words, [512 * t + 256 * g for t in range(PACK)], a_bf[i, g], on_vector)
 
         def quant_a(i, g):
             cols = slice(N * g, N * (g + 1))
@@ -156,46 +151,57 @@ def tile_peptide_mhc_locus_affinity_k7_kernel(
                 in_=c_raw[i][:, cols].rearrange("p (m t b) -> p t m b", t=PACK, b=2),
             )
 
-        def sort_c_scales(i, g):
+        def sort_c_scales(g):
             cols = slice(KP * g, KP * (g + 1))
-            raw = cs_raw0[:, cols] if i == 0 else cs_raw1[:, i - 1, cols]
             nc.vector.tensor_copy(
-                out=c_scales[i][:, cols].rearrange("p (t m) -> p t m", t=PACK),
-                in_=raw.rearrange("p (m t) -> p t m", t=PACK),
+                out=c_scales[0][:, cols].rearrange("p (t m) -> p t m", t=PACK),
+                in_=cs_raw[:, cols].rearrange("p (m t) -> p t m", t=PACK),
             )
 
-        def stage1(u, g, pair):
+        def move_c_scales(i):
+            for quad in range(4):
+                nc.sync.dma_start(
+                    out=c_scales[i][32 * quad : 32 * quad + 4, :].bitcast(I32),
+                    in_=c_scales[0][32 * quad + 4 * i : 32 * quad + 4 * i + 4, :].bitcast(I32),
+                )
+
+        def stage1(u, g, pairs):
             i, h = divmod(u, 2)
-            th[u, g, pair] = work.tile([P, 2, KP], F32, name="th", tag="th", bufs=5)
-            r0 = HALF * h + 2 * P * pair
-            for hi in range(2):
-                bank = psum.tile([P, 2, 2 * P], F32, name="bank", tag="bank", bufs=7)
-                for lo in range(2):
-                    c0 = KP * g + P * (2 * hi + lo)
-                    nc.tensor.matmul_mx(
-                        out=bank[:, lo, :],
-                        lhsT=c_codes[i][:, 2 * c0 : 2 * (c0 + P)].bitcast(FP4X4),
-                        lhsT_scale=c_scales[i][:, c0 : c0 + P],
-                        rhs=x_codes[:, r0 : r0 + 2 * P].bitcast(FP8X4),
-                        rhs_scale=x_scales[:, r0 : r0 + 2 * P],
-                        start=True,
-                        stop=True,
-                    )
+            th[u, g, pairs[0]] = work.tile([P, 2, len(pairs) * KP], F32, name="th", tag="th", bufs=6)
+            banks = []
+            for pair in pairs:
+                r0 = HALF * h + 2 * P * pair
+                for hi in range(2):
+                    bank = psum.tile([P, 2, 2 * P], F32, name="bank", tag="bank", bufs=7)
+                    for lo in range(2):
+                        c0 = KP * g + P * (2 * hi + lo)
+                        nc.tensor.matmul_mx(
+                            out=bank[:, lo, :],
+                            lhsT=c_codes[i][:, 2 * c0 : 2 * (c0 + P)].bitcast(FP4X4),
+                            lhsT_scale=c_scales[i][:, c0 : c0 + P],
+                            rhs=x_codes[:, r0 : r0 + 2 * P].bitcast(FP8X4),
+                            rhs_scale=x_scales[:, r0 : r0 + 2 * P],
+                            start=True,
+                            stop=True,
+                        )
+                    banks.append((pair, hi, bank))
+            for pair, hi, bank in reversed(banks):
                 nc.scalar.activation(
-                    out=th[u, g, pair][:, hi, :].rearrange("p (r e) -> p r e", e=2),
+                    out=th[u, g, pairs[0]][:, hi, KP * (pair - pairs[0]) : KP * (pair - pairs[0] + 1)].rearrange("p (r e) -> p r e", e=2),
                     in_=bank[:].rearrange("p e r -> p r e"),
                     func=ACT.Tanh,
                 )
 
-        def weigh(u, g, pair):
+        def weigh(u, g, pairs):
             i = u // 2
-            if pair == 0:
+            if pairs[0] == 0:
                 h_bf[u, g] = work.tile([P, 2048], BF16, name="h_bf", tag="h_bf", bufs=3, align_bytes=64)
             row = 2 * i + g
+            lo, hi = pairs[0], pairs[-1] + 1
             nc.vector.tensor_tensor(
-                out=h_bf[u, g][:, 1024 * pair : 1024 * (pair + 1)].rearrange("p (r h e) -> p r h e", h=2, e=2),
-                in0=th[u, g, pair][:].rearrange("p h (r e) -> p r h e", e=2),
-                in1=w_ps[:, row : row + 1, :].rearrange("p o (h e) -> p o h e", e=2).to_broadcast([P, 2 * P, 2, 2]),
+                out=h_bf[u, g][:, 1024 * lo : 1024 * hi].rearrange("p (r h e) -> p r h e", h=2, e=2),
+                in0=th[u, g, lo][:].rearrange("p h (r e) -> p r h e", e=2),
+                in1=w_ps[:, row : row + 1, :].rearrange("p o (h e) -> p o h e", e=2).to_broadcast([P, 2 * P * (hi - lo), 2, 2]),
                 op=ALU.mult,
             )
 
@@ -206,13 +212,11 @@ def tile_peptide_mhc_locus_affinity_k7_kernel(
 
         def stage2(u, t):
             i = u // 2
-            if t == 0:
-                sg[u] = work.tile([P, PACK, HALF], F32, name="sg", tag="sg", bufs=2)
-            bank = psum.tile([P, HALF], F32, name="bank", tag="bank", bufs=7)
+            z[u, t] = psum.tile([P, HALF], F32, name="bank", tag="bank", bufs=7)
             for g in range(2):
                 c0 = N * g + P * t
                 nc.tensor.matmul_mx(
-                    out=bank[:],
+                    out=z[u, t][:],
                     lhsT=a_codes[i][:, c0 : c0 + P].bitcast(FP8X4),
                     lhsT_scale=a_scales[i][:, c0 : c0 + P],
                     rhs=h_codes[u, g][:].bitcast(FP8X4),
@@ -220,11 +224,16 @@ def tile_peptide_mhc_locus_affinity_k7_kernel(
                     start=(g == 0),
                     stop=(g == 1),
                 )
-            nc.scalar.activation(out=sg[u][:, t, :], in_=bank[:], func=ACT.Sigmoid, bias=b_sb[:, i, t : t + 1])
+
+        def squash(u, t):
+            i = u // 2
+            if u not in sg:
+                sg[u] = work.tile([P, PACK, HALF], F32, name="sg", tag="sg", bufs=2)
+            nc.scalar.activation(out=sg[u][:, t, :], in_=z[u, t][:], func=ACT.Sigmoid, bias=b_sb[:, i, t : t + 1])
 
         def express(u, t, on_vector):
             i = u // 2
-            if t == 0:
+            if u not in y:
                 y[u] = work.tile([P, PACK, HALF], F32, name="y", tag="y", bufs=3)
             engine = nc.vector if on_vector else nc.gpsimd
             engine.tensor_scalar(
@@ -238,15 +247,14 @@ def tile_peptide_mhc_locus_affinity_k7_kernel(
                     out=y_bf[u][:].rearrange("p (r t) -> p r t", t=PACK), in_=y[u][:].rearrange("p t r -> p r t")
                 )
             else:
-                for c in range(4):
-                    nc.gpsimd.tensor_scalar(
-                        out=y_bf[u][:, KP * c : KP * (c + 1)].rearrange("p (r t) -> p r t", t=PACK),
-                        in0=y[u][:, :, P * c : P * (c + 1)].rearrange("p t r -> p r t"),
-                        scalar1=1.0,
-                        scalar2=0.0,
-                        op0=ALU.mult,
-                        op1=ALU.add,
-                    )
+                nc.gpsimd.tensor_scalar(
+                    out=y_bf[u][:].rearrange("p (r t) -> p r t", t=PACK),
+                    in0=y[u][:].rearrange("p t r -> p r t"),
+                    scalar1=1.0,
+                    scalar2=0.0,
+                    op0=ALU.mult,
+                    op1=ALU.add,
+                )
 
         def quant_y(u):
             cols = slice(HALF * u, HALF * (u + 1))
@@ -266,12 +274,17 @@ def tile_peptide_mhc_locus_affinity_k7_kernel(
         def turn_y(u, chunks, on_vector):
             i, h = divmod(u, 2)
             rows = work.tile([P, len(chunks), N], F32, name="rows", tag="rows", bufs=4)
-            for cc, c in enumerate(chunks):
+            banks = []
+            for c in chunks:
                 bank = psum.tile([P, PACK, P], F32, name="bank", tag="bank", bufs=7)
                 for t in range(PACK):
                     nc.tensor.transpose(bank[:, t, :], y[u][:, t, P * c : P * (c + 1)], ident[:])
+                banks.append(bank)
+            for cc in reversed(range(len(chunks))):
                 leave(
-                    on_vector[cc], rows[:, cc, :].rearrange("r (p t) -> r p t", t=PACK), bank[:].rearrange("r t p -> r p t")
+                    on_vector[cc],
+                    rows[:, cc, :].rearrange("r (p t) -> r p t", t=PACK),
+                    banks[cc][:].rearrange("r t p -> r p t"),
                 )
             r0 = HALF * h + P * chunks[0]
             dst = out_0[i, r0 : r0 + P * len(chunks), :]
@@ -279,97 +292,118 @@ def tile_peptide_mhc_locus_affinity_k7_kernel(
 
         sort_c_codes(0, 0)
         turn_x(0)
-        sort_c_scales(0, 0)
+        sort_c_scales(0)
         quant_x(0)
         turn_x(1)
         nc.vector.tensor_copy(out=w_rows[:], in_=w_raw[:])
         quant_x(1)
         sort_c_codes(0, 1)
-        sort_c_scales(0, 1)
+        sort_c_scales(1)
+        move_c_scales(1)
+        load_c(2)
+        load_a(2)
+        move_c_scales(2)
+        load_c(3)
+        move_c_scales(3)
 
-        stage1(0, 0, 0)
-        stage1(0, 0, 1)
+        stage1(0, 0, [0])
+        stage1(0, 0, [1])
         for t in range(PACK):
             nc.tensor.transpose(w_ps[:, :, t], w_rows[:, t:KP:PACK], ident[:])
-        sort_c_codes(1, 0)
-        weigh(0, 0, 0)
-        stage1(0, 1, 0)
-        weigh(0, 0, 1)
+        weigh(0, 0, [0])
+        weigh(0, 0, [1])
+        stage1(0, 1, [0])
         turn_a(0, 0, False)
+        weigh(0, 1, [0])
+        quant_h(0, 0)
         turn_x(2)
         turn_x(3)
-        weigh(0, 1, 0)
+        stage1(0, 1, [1])
         quant_x(2)
-        quant_h(0, 0)
         quant_x(3)
-        sort_c_scales(1, 0)
+        weigh(0, 1, [1])
         quant_a(0, 0)
-        stage1(0, 1, 1)
         turn_a(0, 1, False)
-        weigh(0, 1, 1)
+        load_a(3)
         nc.vector.tensor_copy(out=b_sb[:], in_=b_raw[:])
         nc.vector.tensor_copy(out=e_sb[:], in_=e_raw[:])
         quant_h(0, 1)
         quant_a(0, 1)
 
         last = UNITS - 1
-        for s in range(1, UNITS):
+        for s in range(1, last):
             nxt_a = divmod(s + 1, 2)
             nxt_c = divmod(s + 3, 2)
-            stage1(s, 0, 0)
-            weigh(s, 0, 0)
-            stage1(s, 0, 1)
-            weigh(s, 0, 1)
-            stage1(s, 1, 0)
-            weigh(s, 1, 0)
-            if s >= 2:
+            stage1(s, 0, [0])
+            stage1(s, 0, [1])
+            weigh(s, 0, [0])
+            weigh(s, 0, [1])
+            stage1(s, 1, [0])
+            weigh(s, 1, [0])
+            if s == 1:
+                sort_c_codes(1, 0)
+                sort_c_codes(1, 1)
+            else:
                 group_y(s - 2, False)
             stage2(s - 1, 0)
+            squash(s - 1, 0)
             express(s - 1, 0, False)
-            if s == 1:
-                turn_a(*nxt_a, False)
-                sort_c_codes(1, 1)
-                sort_c_scales(1, 1)
-            else:
+            if s >= 2:
                 turn_y(s - 2, [0, 1], [False, False])
             stage2(s - 1, 1)
+            squash(s - 1, 1)
             express(s - 1, 1, False)
-            if 2 <= s < last:
-                turn_a(*nxt_a, True)
-            stage1(s, 1, 1)
-            weigh(s, 1, 1)
+            turn_a(*nxt_a, s >= 2)
+            stage1(s, 1, [1])
+            weigh(s, 1, [1])
             stage2(s - 1, 2)
+            squash(s - 1, 2)
             express(s - 1, 2, False)
             if s >= 2:
-                turn_y(s - 2, [2, 3], [False, False])
+                turn_y(s - 2, [2, 3], [s >= 5, False])
             stage2(s - 1, 3)
+            squash(s - 1, 3)
             quant_h(s, 0)
             quant_h(s, 1)
-            if s < last:
-                quant_a(*nxt_a)
+            quant_a(*nxt_a)
             if s >= 2:
                 quant_y(s - 2)
                 store_words(HALF * (s - 2), HALF * (s - 1))
             express(s - 1, 3, True)
             if nxt_c[0] < G:
                 sort_c_codes(*nxt_c)
-                sort_c_scales(*nxt_c)
 
-        store_scales(0, HALF * (last - 1))
+        store_scales(0, HALF * (last - 2))
+        for g in range(2):
+            for pair in range(2):
+                stage1(last, g, [pair])
+                weigh(last, g, [pair])
+        group_y(last - 2, False)
+        quant_h(last, 0)
+        quant_h(last, 1)
+        for t in range(PACK):
+            stage2(last - 1, t)
+            squash(last - 1, t)
+            express(last - 1, t, t >= 2)
+        turn_y(last - 2, [0, 1], [False, False])
+        turn_y(last - 2, [2, 3], [False, False])
+        quant_y(last - 2)
+        store_words(HALF * (last - 2), HALF * (last - 1))
         group_y(last - 1, True)
         stage2(last, 0)
+        squash(last, 0)
         turn_y(last - 1, [0, 1], [False, False])
-        stage2(last, 1)
-        stage2(last, 2)
-        stage2(last, 3)
+        for t in range(1, PACK):
+            stage2(last, t)
+            squash(last, t)
         quant_y(last - 1)
         store_words(HALF * (last - 1), HALF * last)
-        for t in range(4):
+        for t in range(PACK):
             express(last, t, True)
         turn_y(last - 1, [2, 3], [False, False])
         group_y(last, True)
         turn_y(last, [0, 1], [False, False])
         quant_y(last)
         store_words(HALF * last, HALF * UNITS)
-        store_scales(HALF * (last - 1), HALF * UNITS)
-        turn_y(last, [2, 3], [False, True])
+        store_scales(HALF * (last - 2), HALF * UNITS)
+        turn_y(last, [2, 3], [True, False])

from contextlib import ExitStack

import concourse.mybir as mybir
from concourse.masks import make_identity

G, R, K, Q, N = 4, 1024, 512, 1024, 512
FLOPS = 2 * G * R * K * Q + 2 * G * R * Q * N

F32 = mybir.dt.float32
BF16 = mybir.dt.bfloat16
I32 = mybir.dt.int32
U32 = mybir.dt.uint32
U8 = mybir.dt.uint8
FP8X4 = mybir.dt.float8_e4m3fn_x4
FP4X4 = mybir.dt.float4_e2m1fn_x4
ACT = mybir.ActivationFunctionType
ALU = mybir.AluOpType

P = 128
PACK = 4
KP = P * PACK
HALF = 512
UNITS = G * R // HALF


def tile_peptide_mhc_locus_affinity_k7_kernel(
    tc, peptides, contact_words, contact_scales, pocket_weight, alleles, allele_bias, expression, out_0, out_1, out_2
):
    nc = tc.nc
    with ExitStack() as ctx:
        keep = ctx.enter_context(tc.tile_pool(name="keep", bufs=1))
        work = ctx.enter_context(tc.tile_pool(name="work", bufs=2))
        psum = ctx.enter_context(tc.psum_pool(name="psum", bufs=2))
        ctx.enter_context(tc.manual_schedule())

        ident = keep.tile([P, P], F32, name="ident")
        make_identity(nc, ident[:])

        x_raw = [keep.tile([P, 2, K], BF16, name="x_raw%d" % j) for j in range(4)]
        c_raw = [keep.tile([P, 2 * Q], U8, name="c_raw%d" % i) for i in range(G)]
        cs_raw = keep.tile([P, Q], U8, name="cs_raw")
        a_raw = {}
        w_raw = keep.tile([P, KP], BF16, name="w_raw")
        w_rows = keep.tile([P, KP], F32, name="w_rows")
        b_raw = keep.tile([P, G, PACK], BF16, name="b_raw")
        e_raw = keep.tile([P, G, PACK], BF16, name="e_raw")
        w_ps = psum.tile([P, P, PACK], F32, name="w_ps", tag="w_ps", bufs=1)
        b_sb = keep.tile([P, G, PACK], F32, name="b_sb")
        e_sb = keep.tile([P, G, PACK], F32, name="e_sb")
        warm = keep.tile([P, 1], F32, name="warm")

        x_codes = keep.tile([P, R], U32, name="x_codes", align_bytes=64)
        x_scales = keep.tile([P, R], U8, name="x_scales", align_bytes=64)
        c_codes = [keep.tile([P, 2 * Q], U8, name="c_codes%d" % i, align_bytes=64) for i in range(G)]
        c_scales = [keep.tile([P, Q], U8, name="c_scales%d" % i, align_bytes=64) for i in range(G)]
        a_codes = [keep.tile([P, 2 * N], U32, name="a_codes%d" % i, align_bytes=64) for i in range(G)]
        a_scales = [keep.tile([P, 2 * N], U8, name="a_scales%d" % i, align_bytes=64) for i in range(G)]
        y_codes = keep.tile([P, G * R], U32, name="y_codes", align_bytes=64)
        y_scales = keep.tile([P, G * R], U8, name="y_scales", align_bytes=64)

        nc.vector.memset(cs_raw[:].bitcast(I32), 0)
        nc.vector.memset(w_raw[:], 0.0)
        for i in range(1, G):
            nc.vector.memset(c_scales[i][:].bitcast(I32), 0)

        def load_x(j):
            rows = peptides[256 * j : 256 * (j + 1), :]
            nc.sync.dma_start(out=x_raw[j][:], in_=rows.rearrange("(c p) k -> p c k", p=P))

        def load_c(i):
            nc.sync.dma_start(out=c_raw[i][:].bitcast(I32), in_=contact_words[i].bitcast(I32))

        def load_a(i):
            a_raw[i] = work.tile([P, PACK, Q], BF16, name="a_raw", tag="a_raw", bufs=3)
            nc.sync.dma_start(out=a_raw[i][:], in_=alleles[i].rearrange("(m t) q -> m t q", t=PACK))

        load_x(0)
        load_c(0)
        for quad in range(4):
            nc.scalar.dma_start(
                out=cs_raw[32 * quad : 32 * quad + 4 * G, :].bitcast(I32),
                in_=contact_scales[:, 4 * quad : 4 * quad + 4, :].bitcast(I32),
            )
        load_x(1)
        nc.sync.dma_start(out=w_raw[0 : 2 * G, :], in_=pocket_weight.rearrange("i (g q) -> (i g) q", g=2))
        load_a(0)
        load_c(1)
        load_x(2)
        load_x(3)
        nc.sync.dma_start(out=b_raw[:], in_=allele_bias.rearrange("i (p t) -> p i t", t=PACK))
        nc.sync.dma_start(out=e_raw[:], in_=expression.rearrange("i (p t) -> p i t", t=PACK))
        load_a(1)

        nc.scalar.activation(out=warm[:], in_=ident[:, 0:1], func=ACT.Sigmoid)

        x_bf = {}
        a_bf = {}
        th = {}
        h_bf = {}
        h_codes = {}
        h_scales = {}
        z = {}
        sg = {}
        y = {}
        y_bf = {}

        def leave(on_vector, out, in_):
            if on_vector:
                nc.vector.tensor_copy(out=out, in_=in_)
            else:
                nc.scalar.copy(out=out, in_=in_)

        def turn_words(words, firsts, grouped, on_vector):
            banks = []
            for j in range(len(firsts) // 2):
                bank = psum.tile([P, 2, 2, P], F32, name="bank", tag="bank", bufs=7)
                for x in range(2):
                    for u in range(2):
                        lo = firsts[2 * j + x]
                        nc.tensor.transpose(bank[:, x, u, :], words[:, lo + u : lo + 256 : 2], ident[:])
                banks.append(bank)
            for j in reversed(range(len(banks))):
                leave(
                    on_vector,
                    grouped[:, 1024 * j : 1024 * (j + 1)].bitcast(F32).rearrange("p (x m u) -> p x m u", x=2, u=2),
                    banks[j][:].rearrange("p x u m -> p x m u"),
                )

        def turn_x(j):
            x_bf[j] = work.tile([P, 1024], BF16, name="x_bf", tag="x_bf", bufs=2, align_bytes=64)
            words = x_raw[j][:].rearrange("p c k -> p (c k)").bitcast(F32)
            turn_words(words, [0, 256], x_bf[j], False)

        def quant_x(j):
            cols = slice(256 * j, 256 * (j + 1))
            nc.vector.quantize_mx(out=x_codes[:, cols].bitcast(FP8X4), scales=x_scales[:, cols], in_=x_bf[j][:])

        def turn_a(i, g, on_vector):
            a_bf[i, g] = work.tile([P, 2048], BF16, name="a_bf", tag="a_bf", bufs=2, align_bytes=64)
            words = a_raw[i][:].rearrange("p t q -> p (t q)").bitcast(F32)
            turn_words(words, [512 * t + 256 * g for t in range(PACK)], a_bf[i, g], on_vector)

        def quant_a(i, g):
            cols = slice(N * g, N * (g + 1))
            nc.vector.quantize_mx(out=a_codes[i][:, cols].bitcast(FP8X4), scales=a_scales[i][:, cols], in_=a_bf[i, g][:])

        def sort_c_codes(i, g):
            cols = slice(1024 * g, 1024 * (g + 1))
            nc.vector.tensor_copy(
                out=c_codes[i][:, cols].rearrange("p (t m b) -> p t m b", t=PACK, b=2),
                in_=c_raw[i][:, cols].rearrange("p (m t b) -> p t m b", t=PACK, b=2),
            )

        def sort_c_scales(g):
            cols = slice(KP * g, KP * (g + 1))
            nc.vector.tensor_copy(
                out=c_scales[0][:, cols].rearrange("p (t m) -> p t m", t=PACK),
                in_=cs_raw[:, cols].rearrange("p (m t) -> p t m", t=PACK),
            )

        def move_c_scales(i):
            for quad in range(4):
                nc.sync.dma_start(
                    out=c_scales[i][32 * quad : 32 * quad + 4, :].bitcast(I32),
                    in_=c_scales[0][32 * quad + 4 * i : 32 * quad + 4 * i + 4, :].bitcast(I32),
                )

        def stage1(u, g, pairs):
            i, h = divmod(u, 2)
            th[u, g, pairs[0]] = work.tile([P, 2, len(pairs) * KP], F32, name="th", tag="th", bufs=6)
            banks = []
            for pair in pairs:
                r0 = HALF * h + 2 * P * pair
                for hi in range(2):
                    bank = psum.tile([P, 2, 2 * P], F32, name="bank", tag="bank", bufs=7)
                    for lo in range(2):
                        c0 = KP * g + P * (2 * hi + lo)
                        nc.tensor.matmul_mx(
                            out=bank[:, lo, :],
                            lhsT=c_codes[i][:, 2 * c0 : 2 * (c0 + P)].bitcast(FP4X4),
                            lhsT_scale=c_scales[i][:, c0 : c0 + P],
                            rhs=x_codes[:, r0 : r0 + 2 * P].bitcast(FP8X4),
                            rhs_scale=x_scales[:, r0 : r0 + 2 * P],
                            start=True,
                            stop=True,
                        )
                    banks.append((pair, hi, bank))
            for pair, hi, bank in reversed(banks):
                nc.scalar.activation(
                    out=th[u, g, pairs[0]][:, hi, KP * (pair - pairs[0]) : KP * (pair - pairs[0] + 1)].rearrange("p (r e) -> p r e", e=2),
                    in_=bank[:].rearrange("p e r -> p r e"),
                    func=ACT.Tanh,
                )

        def weigh(u, g, pairs):
            i = u // 2
            if pairs[0] == 0:
                h_bf[u, g] = work.tile([P, 2048], BF16, name="h_bf", tag="h_bf", bufs=3, align_bytes=64)
            row = 2 * i + g
            lo, hi = pairs[0], pairs[-1] + 1
            nc.vector.tensor_tensor(
                out=h_bf[u, g][:, 1024 * lo : 1024 * hi].rearrange("p (r h e) -> p r h e", h=2, e=2),
                in0=th[u, g, lo][:].rearrange("p h (r e) -> p r h e", e=2),
                in1=w_ps[:, row : row + 1, :].rearrange("p o (h e) -> p o h e", e=2).to_broadcast([P, 2 * P * (hi - lo), 2, 2]),
                op=ALU.mult,
            )

        def quant_h(u, g):
            h_codes[u, g] = work.tile([P, HALF], U32, name="h_codes", tag="h_codes", bufs=4, align_bytes=64)
            h_scales[u, g] = work.tile([P, HALF], U8, name="h_scales", tag="h_scales", bufs=4, align_bytes=64)
            nc.vector.quantize_mx(out=h_codes[u, g][:].bitcast(FP8X4), scales=h_scales[u, g][:], in_=h_bf[u, g][:])

        def stage2(u, t):
            i = u // 2
            z[u, t] = psum.tile([P, HALF], F32, name="bank", tag="bank", bufs=7)
            for g in range(2):
                c0 = N * g + P * t
                nc.tensor.matmul_mx(
                    out=z[u, t][:],
                    lhsT=a_codes[i][:, c0 : c0 + P].bitcast(FP8X4),
                    lhsT_scale=a_scales[i][:, c0 : c0 + P],
                    rhs=h_codes[u, g][:].bitcast(FP8X4),
                    rhs_scale=h_scales[u, g][:],
                    start=(g == 0),
                    stop=(g == 1),
                )

        def squash(u, t):
            i = u // 2
            if u not in sg:
                sg[u] = work.tile([P, PACK, HALF], F32, name="sg", tag="sg", bufs=2)
            nc.scalar.activation(out=sg[u][:, t, :], in_=z[u, t][:], func=ACT.Sigmoid, bias=b_sb[:, i, t : t + 1])

        def express(u, t, on_vector):
            i = u // 2
            if u not in y:
                y[u] = work.tile([P, PACK, HALF], F32, name="y", tag="y", bufs=3)
            engine = nc.vector if on_vector else nc.gpsimd
            engine.tensor_scalar(
                out=y[u][:, t, :], in0=sg[u][:, t, :], scalar1=e_sb[:, i, t : t + 1], scalar2=0.0, op0=ALU.mult, op1=ALU.add
            )

        def group_y(u, on_vector):
            y_bf[u] = work.tile([P, 2048], BF16, name="y_bf", tag="y_bf", bufs=2, align_bytes=64)
            if on_vector:
                nc.vector.tensor_copy(
                    out=y_bf[u][:].rearrange("p (r t) -> p r t", t=PACK), in_=y[u][:].rearrange("p t r -> p r t")
                )
            else:
                nc.gpsimd.tensor_scalar(
                    out=y_bf[u][:].rearrange("p (r t) -> p r t", t=PACK),
                    in0=y[u][:].rearrange("p t r -> p r t"),
                    scalar1=1.0,
                    scalar2=0.0,
                    op0=ALU.mult,
                    op1=ALU.add,
                )

        def quant_y(u):
            cols = slice(HALF * u, HALF * (u + 1))
            nc.vector.quantize_mx(out=y_codes[:, cols].bitcast(FP8X4), scales=y_scales[:, cols], in_=y_bf[u][:])

        def store_words(lo, hi):
            words = out_1[0].rearrange("p m t -> p (m t)")[:, PACK * lo : PACK * hi]
            nc.sync.dma_start(out=words.bitcast(I32), in_=y_codes[:, lo:hi].bitcast(I32))

        def store_scales(lo, hi):
            for quad in range(4):
                nc.sync.dma_start(
                    out=out_2[0, 4 * quad : 4 * quad + 4, lo:hi].bitcast(I32),
                    in_=y_scales[32 * quad : 32 * quad + 4, lo:hi].bitcast(I32),
                )

        def turn_y(u, chunks, on_vector):
            i, h = divmod(u, 2)
            rows = work.tile([P, len(chunks), N], F32, name="rows", tag="rows", bufs=4)
            banks = []
            for c in chunks:
                bank = psum.tile([P, PACK, P], F32, name="bank", tag="bank", bufs=7)
                for t in range(PACK):
                    nc.tensor.transpose(bank[:, t, :], y[u][:, t, P * c : P * (c + 1)], ident[:])
                banks.append(bank)
            for cc in reversed(range(len(chunks))):
                leave(
                    on_vector[cc],
                    rows[:, cc, :].rearrange("r (p t) -> r p t", t=PACK),
                    banks[cc][:].rearrange("r t p -> r p t"),
                )
            r0 = HALF * h + P * chunks[0]
            dst = out_0[i, r0 : r0 + P * len(chunks), :]
            nc.sync.dma_start(out=dst.rearrange("(c p) a -> p c a", p=P), in_=rows[:])

        sort_c_codes(0, 0)
        turn_x(0)
        sort_c_scales(0)
        quant_x(0)
        turn_x(1)
        nc.vector.tensor_copy(out=w_rows[:], in_=w_raw[:])
        quant_x(1)
        sort_c_codes(0, 1)
        sort_c_scales(1)
        move_c_scales(1)
        load_c(2)
        load_a(2)
        move_c_scales(2)
        load_c(3)
        move_c_scales(3)

        stage1(0, 0, [0])
        stage1(0, 0, [1])
        for t in range(PACK):
            nc.tensor.transpose(w_ps[:, :, t], w_rows[:, t:KP:PACK], ident[:])
        weigh(0, 0, [0])
        weigh(0, 0, [1])
        stage1(0, 1, [0])
        turn_a(0, 0, False)
        weigh(0, 1, [0])
        quant_h(0, 0)
        turn_x(2)
        turn_x(3)
        stage1(0, 1, [1])
        quant_x(2)
        quant_x(3)
        weigh(0, 1, [1])
        quant_a(0, 0)
        turn_a(0, 1, False)
        load_a(3)
        nc.vector.tensor_copy(out=b_sb[:], in_=b_raw[:])
        nc.vector.tensor_copy(out=e_sb[:], in_=e_raw[:])
        quant_h(0, 1)
        quant_a(0, 1)

        last = UNITS - 1
        for s in range(1, last):
            nxt_a = divmod(s + 1, 2)
            nxt_c = divmod(s + 3, 2)
            stage1(s, 0, [0])
            stage1(s, 0, [1])
            weigh(s, 0, [0])
            weigh(s, 0, [1])
            stage1(s, 1, [0])
            weigh(s, 1, [0])
            if s == 1:
                sort_c_codes(1, 0)
                sort_c_codes(1, 1)
            else:
                group_y(s - 2, False)
            stage2(s - 1, 0)
            squash(s - 1, 0)
            express(s - 1, 0, False)
            if s >= 2:
                turn_y(s - 2, [0, 1], [False, False])
            stage2(s - 1, 1)
            squash(s - 1, 1)
            express(s - 1, 1, False)
            turn_a(*nxt_a, s >= 2)
            stage1(s, 1, [1])
            weigh(s, 1, [1])
            stage2(s - 1, 2)
            squash(s - 1, 2)
            express(s - 1, 2, False)
            if s >= 2:
                turn_y(s - 2, [2, 3], [s >= 5, False])
            stage2(s - 1, 3)
            squash(s - 1, 3)
            quant_h(s, 0)
            quant_h(s, 1)
            quant_a(*nxt_a)
            if s >= 2:
                quant_y(s - 2)
                store_words(HALF * (s - 2), HALF * (s - 1))
            express(s - 1, 3, True)
            if nxt_c[0] < G:
                sort_c_codes(*nxt_c)

        store_scales(0, HALF * (last - 2))
        for g in range(2):
            for pair in range(2):
                stage1(last, g, [pair])
                weigh(last, g, [pair])
        group_y(last - 2, False)
        quant_h(last, 0)
        quant_h(last, 1)
        for t in range(PACK):
            stage2(last - 1, t)
            squash(last - 1, t)
            express(last - 1, t, t >= 2)
        turn_y(last - 2, [0, 1], [False, False])
        turn_y(last - 2, [2, 3], [False, False])
        quant_y(last - 2)
        store_words(HALF * (last - 2), HALF * (last - 1))
        group_y(last - 1, True)
        stage2(last, 0)
        squash(last, 0)
        turn_y(last - 1, [0, 1], [False, False])
        for t in range(1, PACK):
            stage2(last, t)
            squash(last, t)
        quant_y(last - 1)
        store_words(HALF * (last - 1), HALF * last)
        for t in range(PACK):
            express(last, t, True)
        turn_y(last - 1, [2, 3], [False, False])
        group_y(last, True)
        turn_y(last, [0, 1], [False, False])
        quant_y(last)
        store_words(HALF * last, HALF * UNITS)
        store_scales(HALF * (last - 2), HALF * UNITS)
        turn_y(last, [2, 3], [True, False])
